import numpy as np
import ml_dtypes


def mxq(x, axis, fmt="e4m3"):
    dtype, down = {"e4m3": (ml_dtypes.float8_e4m3fn, 7), "e5m2": (ml_dtypes.float8_e5m2, 14)}[fmt]
    v = np.moveaxis(np.asarray(x, np.float32).astype(ml_dtypes.bfloat16).astype(np.float64), axis, -1)
    blocks = v.reshape(v.shape[:-1] + (-1, 32))
    amax = np.abs(blocks).max(-1, keepdims=True)
    byte = np.maximum(np.where(amax > 0, np.frexp(amax)[1] - 1 + 127, 0) - down, 1)
    scale = np.exp2(byte - 127.0)
    codes = (blocks / scale).astype(np.float32).astype(dtype).astype(np.float64)
    return np.moveaxis((codes * scale).reshape(v.shape), -1, axis)


WIDE = False


def mx_kscale(k):
    if not WIDE:
        return np.ones(k)
    levels = np.array([10, -10, 5, -5, 0])
    if k % 512:
        return np.exp2(np.random.permutation(np.resize(levels, k // 32))).repeat(32)
    a = np.empty((k // 512, 16))
    for p in range(k // 512):
        a[p, :8] = np.random.permutation(np.resize(levels, 8))
        for g in range(8):
            far = levels[np.abs(levels - a[p, g]) >= 10]
            a[p, g + 8] = far[np.random.randint(len(far))]
    return np.exp2(a.ravel()).repeat(32)


def f64(x):
    return np.asarray(x).astype(np.float64)


def striped(idx):
    return np.tile(idx.reshape(-1, 16).T, (8, 1)).astype(np.uint16)


def unstriped(offs):
    return offs[:16].T.reshape(-1).astype(np.int64)


E2M1 = np.array([0.0, 0.5, 1.0, 1.5, 2.0, 3.0, 4.0, 6.0, -0.0, -0.5, -1.0, -1.5, -2.0, -3.0, -4.0, -6.0])


def pack_weight(w, fmt):
    k, n = w.shape
    w = f64(np.asarray(w, np.float32).astype(ml_dtypes.bfloat16)).reshape(k // 32, 32, n)
    amax = np.abs(w).max(1)
    if fmt == "e4m3":
        byte = np.frexp(amax)[1] - 1 + 127 - 7
    else:
        mant, ex = np.frexp(amax / 6.0)
        byte = np.where(mant > 0.5, ex, ex - 1) + 127
    byte = np.clip(np.where(amax > 0, byte, 1), 1, 254)
    scaled = (w * np.exp2(127.0 - byte)[:, None, :]).reshape(k, n).astype(np.float32)
    by_word = np.ascontiguousarray(scaled.reshape(k // 512, 128, 4, n).transpose(0, 1, 3, 2))
    if fmt == "e4m3":
        words = by_word.astype(ml_dtypes.float8_e4m3fn).view(np.uint8)
    else:
        c = by_word.astype(ml_dtypes.float4_e2m1fn).view(np.uint8) & 0xF
        words = (c[..., 0::2] | (c[..., 1::2] << 4)).reshape(k // 512, 128, 2 * n)
    return np.ascontiguousarray(words), np.ascontiguousarray(byte.astype(np.uint8).reshape(k // 512, 16, n))


def unpack_weight(words, scales, fmt):
    g, _, n = scales.shape
    words = np.ascontiguousarray(words).reshape(g, 128, n, -1)
    if fmt == "e4m3":
        vals = words.view(ml_dtypes.float8_e4m3fn).astype(np.float64)
    else:
        nib = np.empty((g, 128, n, 4), np.uint8)
        nib[..., 0::2] = words & 0xF
        nib[..., 1::2] = words >> 4
        vals = E2M1[nib]
    vals = vals * np.repeat(np.exp2(scales.astype(np.float64) - 127.0), 8, axis=1)[..., None]
    return vals.transpose(0, 1, 3, 2).reshape(g * 512, n)


def gelu(v):
    return 0.5 * v * (1.0 + np.tanh(np.sqrt(2.0 / np.pi) * (v + 0.044715 * v**3)))


K, R, M, N, T, S, P = 1024, 512, 1024, 384, 4096, 1024, 512


def setup_inputs():
    n = np.random.standard_normal
    s = mx_kscale(K)[:, None]
    ur = mx_kscale(R)[:, None]
    um = mx_kscale(M)[:, None]
    d = {}
    d["tab_words"], d["tab_scales"] = pack_weight(n((K, T)) * s, "e2m1")
    d["offs"] = striped(np.random.permutation(T)[:S])
    d["pos1"] = striped(np.random.permutation(S)[:P])
    d["pos2"] = striped(np.random.permutation(S)[:P])
    d["w1"] = (1.5 * n((K, R)) / K ** 0.5 / s).astype(np.float32)
    d["gain"] = (np.exp(0.3 * n(R)) * ur[:, 0]).astype(np.float32)
    d["w2_words"], d["w2_scales"] = pack_weight(n((K, M)) / K ** 0.5 / s * um.T, "e4m3")
    d["w3"] = (n((R, N)) / R ** 0.5 / ur).astype(np.float32)
    d["w4_words"], d["w4_scales"] = pack_weight(n((M, N)) / M ** 0.5 / um, "e2m1")
    return d


def reference(tab_words, tab_scales, offs, pos1, pos2, w1, gain, w2_words, w2_scales, w3, w4_words, w4_scales):
    v = unpack_weight(tab_words, tab_scales, "e2m1")[:, unstriped(offs)]
    w2 = unpack_weight(w2_words, w2_scales, "e4m3")
    w4 = unpack_weight(w4_words, w4_scales, "e2m1")
    den = f64(gain)[:, None] * np.tanh(mxq(f64(w1), 0, "e4m3").T @ v)
    dep = np.maximum(w2.T @ v, 0.0)
    diff = den[:, unstriped(pos1)] - den[:, unstriped(pos2)]
    both = dep[:, unstriped(pos1)] + dep[:, unstriped(pos2)]
    drive = mxq(f64(w3), 0, "e4m3").T @ mxq(diff, 0, "e4m3")
    level = w4.T @ mxq(both, 0, "e4m3")
    return drive * level + drive

@@ -1,0 +1,262 @@
+from contextlib import ExitStack
+
+import concourse.mybir as mybir
+from concourse.masks import make_identity
+
+K, R, M, N, T, S, PAIRS = 1024, 512, 1024, 384, 4096, 1024, 512
+FLOPS = 2 * K * (R + M) * S + 2 * (R + M) * N * PAIRS
+
+F32 = mybir.dt.float32
+BF16 = mybir.dt.bfloat16
+I32 = mybir.dt.int32
+U32 = mybir.dt.uint32
+U16 = mybir.dt.uint16
+U8 = mybir.dt.uint8
+E4M3 = mybir.dt.float8_e4m3fn_x4
+E2M1 = mybir.dt.float4_e2m1fn_x4
+ACT = mybir.ActivationFunctionType
+ALU = mybir.AluOpType
+
+P = 128
+BANK = 512
+HALVES = S // BANK
+SPARE_ROW = 112
+PAIR_CHUNKS = (256, 128, 128)
+
+
+def tile_list_saltpond_transfer_features_kernel(
+    tc, tab_words, tab_scales, offs, pos1, pos2, w1, gain, w2_words, w2_scales, w3, w4_words, w4_scales, out
+):
+    nc = tc.nc
+    with ExitStack() as ctx:
+        keep = ctx.enter_context(tc.tile_pool(name="keep", bufs=1))
+        ring = ctx.enter_context(tc.tile_pool(name="ring", bufs=8))
+        psum = ctx.enter_context(tc.psum_pool(name="psum", bufs=2))
+
+        def held(shape, dtype, name, tag=None):
+            return keep.tile(shape, dtype, name=name, tag=tag or name, align_bytes=64)
+
+        offs_sb = keep.tile([P, S // 16], U16, name="offs_sb")
+        pos1_sb = keep.tile([P, PAIRS // 16], U16, name="pos1_sb")
+        pos2_sb = keep.tile([P, PAIRS // 16], U16, name="pos2_sb")
+        nc.sync.dma_start(offs_sb[:], offs)
+
+        tab_sc = held([P, T], U8, "tab_sc", "early0")
+        nc.sync.dma_start(tab_sc[SPARE_ROW:P, :].bitcast(I32), tab_scales[1].bitcast(I32))
+        nc.vector.memset(tab_sc[0:SPARE_ROW, :].bitcast(I32), 0)
+        for q in range(4):
+            nc.scalar.dma_start(tab_sc[32 * q : 32 * q + 4, :].bitcast(I32), tab_scales[0, 4 * q : 4 * q + 4, :].bitcast(I32))
+
+        tab_w = [held([P, T], U16, f"tab_w{a}", f"early{a + 1}") for a in range(2)]
+        nc.sync.dma_start(tab_w[0][:].bitcast(I32), tab_words[0].bitcast(I32))
+        nc.sync.dma_start(pos1_sb[:], pos1)
+        nc.sync.dma_start(pos2_sb[:], pos2)
+        nc.sync.dma_start(tab_w[1][:].bitcast(I32), tab_words[1].bitcast(I32))
+
+        w2_c = [held([P, 2, BANK], U32, f"w2_c{g}") for g in range(2)]
+        w2_view = w2_words.rearrange("a p c i -> p a (c i)")
+        for g in range(2):
+            nc.sync.dma_start(w2_c[g][:].bitcast(I32), w2_view[:, :, 4 * BANK * g : 4 * BANK * (g + 1)].bitcast(I32))
+
+        def load_scale_planes(planes, scales):
+            nc.gpsimd.memset(planes[:].bitcast(I32), 0)
+            for q in range(4):
+                nc.gpsimd.dma_start(
+                    planes[32 * q : 32 * q + 4, :, :].bitcast(I32),
+                    scales[:, 4 * q : 4 * q + 4, :].rearrange("a r c -> r a c").bitcast(I32),
+                )
+
+        w2_s = held([P, 2, M], U8, "w2_s")
+        load_scale_planes(w2_s, w2_scales)
+        ident = held([P, P], F32, "ident")
+        make_identity(nc, ident[:])
+        w4_s = held([P, 2, N], U8, "w4_s")
+        load_scale_planes(w4_s, w4_scales)
+        gain_sb = held([P, 4], F32, "gain_sb")
+        nc.gpsimd.dma_start(gain_sb[:], gain.rearrange("(p t) -> p t", t=4))
+        w4_c = held([P, 2, 2 * N], U8, "w4_c")
+        nc.gpsimd.dma_start(w4_c[:].bitcast(I32), w4_words.rearrange("a p c -> p a c").bitcast(I32))
+
+        v_s = [held([P, S], U8, f"v_s{a}") for a in range(2)]
+        nc.vector.memset(v_s[1][:].bitcast(I32), 0)
+        nc.vector.tensor_copy(v_s[0][:], tab_sc[:].indirect(offs_sb[:]))
+        for q in range(4):
+            nc.scalar.dma_start(
+                v_s[1][32 * q : 32 * q + 4, :].bitcast(I32),
+                v_s[0][SPARE_ROW + 4 * q : SPARE_ROW + 4 * q + 4, :].bitcast(I32),
+            )
+        v_c = [[held([P, BANK], U16, f"v_c{a}{h}") for h in range(HALVES)] for a in range(2)]
+        for a in range(2):
+            for h in range(HALVES):
+                nc.vector.tensor_copy(v_c[a][h][:], tab_w[a][:].indirect(offs_sb[:, 32 * h : 32 * (h + 1)]))
+
+        w3_raw = held([P, 4, N], F32, "w3_raw", "early0")
+        nc.sync.dma_start(w3_raw[:], w3.rearrange("(p j) n -> p j n", j=4))
+        w1_raw = [held([P, 4, R], F32, f"w1_raw{a}", f"early{a + 1}") for a in range(2)]
+        for a in range(2):
+            nc.sync.dma_start(w1_raw[a][:], w1[512 * a : 512 * (a + 1), :].rearrange("(p j) c -> p j c", j=4))
+
+        w3_b = held([P, 4 * N], BF16, "w3_b")
+        w3_c = held([P, N], U32, "w3_c")
+        w3_s = held([P, N], U8, "w3_s")
+        nc.vector.tensor_copy(w3_b[:].rearrange("p (n j) -> p n j", j=4), w3_raw[:].rearrange("p j n -> p n j"))
+        for c0, c1 in ((0, 256), (256, N)):
+            nc.vector.quantize_mx(w3_c[:, c0:c1].bitcast(E4M3), w3_s[:, c0:c1], w3_b[:, 4 * c0 : 4 * c1])
+
+        w1_b = [held([P, 4 * R], BF16, f"w1_b{a}") for a in range(2)]
+        w1_c = [held([P, R], U32, f"w1_c{a}") for a in range(2)]
+        w1_s = [held([P, R], U8, f"w1_s{a}") for a in range(2)]
+
+        def round_w1(a, half):
+            rows = slice(64 * half, 64 * (half + 1))
+            nc.scalar.copy(
+                w1_b[a][:].rearrange("p (t m j) -> p m j t", t=4, j=4)[:, rows],
+                w1_raw[a][:].rearrange("p j (m t) -> p m j t", t=4)[:, rows],
+            )
+            if half == 1:
+                nc.vector.quantize_mx(w1_c[a][:].bitcast(E4M3), w1_s[a][:], w1_b[a][:])
+
+        def first_stage(name, codes, scales, func):
+            window = held([P, S], F32, name)
+            for h in range(HALVES):
+                cols = slice(BANK * h, BANK * (h + 1))
+                acc = psum.tile([P, BANK], F32, name="acc", tag="acc", bufs=4)
+                for a in range(2):
+                    nc.tensor.matmul_mx(
+                        acc[:], codes[a].bitcast(E4M3), scales[a], v_c[a][h][:].bitcast(E2M1), v_s[a][:, cols],
+                        start=(a == 0), stop=(a == 1),
+                    )
+                nc.scalar.activation(window[:, cols], acc[:], func)
+            return window
+
+        def dep_window(b):
+            g, c0 = b // 4, P * (b % 4)
+            return first_stage(
+                f"dep{b}",
+                [w2_c[g][:, a, c0 : c0 + P] for a in range(2)],
+                [w2_s[:, a, P * b : P * (b + 1)] for a in range(2)],
+                ACT.Relu,
+            )
+
+        def den_window(t):
+            cols = slice(P * t, P * (t + 1))
+            return first_stage(f"den{t}", [w1_c[a][:, cols] for a in range(2)], [w1_s[a][:, cols] for a in range(2)], ACT.Tanh)
+
+        def pick_dep(window):
+            picks = []
+            for pos_sb in (pos1_sb, pos2_sb):
+                pick = ring.tile([P, PAIRS], F32, name="pick", tag="pick")
+                nc.vector.tensor_copy(pick[:], window[:].indirect(pos_sb[:]))
+                picks.append(pick)
+            return picks
+
+        both_t = [held([P, 4 * BANK], BF16, f"both_t{g}") for g in range(2)]
+        both_b = [held([P, 4 * PAIRS], BF16, f"both_b{g}") for g in range(2)]
+        both_c = [held([P, PAIRS], U32, f"both_c{g}") for g in range(2)]
+        both_s = [held([P, PAIRS], U8, f"both_s{g}") for g in range(2)]
+
+        def sum_picks(b, picks):
+            bank = psum.tile([P, BANK], F32, name="total", tag="total")
+            for jb in range(4):
+                cols = slice(P * jb, P * (jb + 1))
+                for i in range(2):
+                    nc.tensor.matmul(bank[:, cols], picks[i][:, cols], ident[:], start=(i == 0), stop=(i == 1), is_transpose=True)
+            rows = slice(32 * (b % 4), 32 * (b % 4 + 1))
+            nc.scalar.copy(
+                both_t[b // 4][:].rearrange("p (jb u q e) -> p jb u q e", jb=4, u=2, e=2)[:, :, :, rows, :],
+                bank[:].rearrange("p (jb q u e) -> p jb u q e", jb=4, u=2, e=2),
+            )
+
+        def turn_back(g):
+            words = both_t[g][:].bitcast(F32)
+            dst = both_b[g][:].bitcast(F32)
+            for half in range(2):
+                bank = psum.tile([P, BANK], F32, name="back", tag="back")
+                for i in range(4):
+                    nc.tensor.transpose(bank[:, P * i : P * (i + 1)], words[:, P * (4 * half + i) : P * (4 * half + i + 1)], ident[:])
+                nc.scalar.copy(
+                    dst[:, BANK * half : BANK * (half + 1)].rearrange("p (jb j u) -> p jb j u", jb=2, u=2),
+                    bank[:].rearrange("p (jb u j) -> p jb j u", jb=2, u=2),
+                )
+            nc.vector.quantize_mx(both_c[g][:].bitcast(E4M3), both_s[g][:], both_b[g][:])
+
+        level = held([P, 3, PAIRS], F32, "level")
+
+        def level_product():
+            for nt in range(3):
+                acc = psum.tile([P, BANK], F32, name="acc", tag="acc", bufs=4)
+                for g in range(2):
+                    nc.tensor.matmul_mx(
+                        acc[:], w4_c[:, g, 2 * P * nt : 2 * P * (nt + 1)].bitcast(E2M1), w4_s[:, g, P * nt : P * (nt + 1)],
+                        both_c[g][:].bitcast(E4M3), both_s[g][:], start=(g == 0), stop=(g == 1),
+                    )
+                nc.scalar.copy(level[:, nt, :], acc[:])
+
+        def pick_den(den, j0, width):
+            entries = slice(j0 // 16, (j0 + width) // 16)
+            rounded = held([P, 4, width], BF16, f"diff_r{j0}")
+            for t in range(4):
+                taker = ring.tile([P, width], F32, name="taker", tag="taker", bufs=4)
+                diff = ring.tile([P, width], F32, name="diff", tag="diff", bufs=4)
+                nc.vector.tensor_copy(taker[:], den[t][:].indirect(pos2_sb[:, entries]))
+                nc.vector.tensor_tensor(diff[:], den[t][:].indirect(pos1_sb[:, entries]), taker[:], ALU.subtract)
+                nc.scalar.activation(rounded[:, t, :], diff[:], ACT.Copy, scale=gain_sb[:, t : t + 1])
+            return rounded
+
+        out_view = out.rearrange("(nt p) j -> p nt j", p=P)
+
+        def finish(rounded, c0, j0, last):
+            woven = held([P, 4 * P], BF16, f"diff_b{j0}")
+            codes = held([P, P], U32, f"diff_c{j0}")
+            scales = held([P, P], U8, f"diff_s{j0}")
+            src = rounded[:, :, c0 : c0 + P].rearrange("p t j -> p j t")
+            dst = woven[:].rearrange("p (j t) -> p j t", t=4)
+            if last:
+                nc.vector.tensor_copy(dst, src)
+            else:
+                nc.scalar.copy(dst, src)
+            nc.vector.quantize_mx(codes[:].bitcast(E4M3), scales[:], woven[:])
+            tag = "total" if (j0 // P) % 2 == 0 else "back"
+            drive = psum.tile([P, BANK], F32, name=tag, tag=tag)
+            for nt in range(3):
+                cols = slice(P * nt, P * (nt + 1))
+                nc.tensor.matmul_mx(
+                    drive[:, cols], w3_c[:, cols].bitcast(E4M3), w3_s[:, cols], codes[:].bitcast(E4M3), scales[:], start=True, stop=True
+                )
+            result = held([P, 3, P], F32, f"result{j0}")
+            nc.vector.scalar_tensor_tensor(
+                result[:], level[:, :, j0 : j0 + P], 1.0, drive[:, 0 : 3 * P].rearrange("p (nt j) -> p nt j", nt=3), ALU.add, ALU.mult
+            )
+            nc.sync.dma_start(out_view[:, :, j0 : j0 + P], result[:])
+
+        dep = [dep_window(0), dep_window(1), dep_window(2)]
+        picks = [pick_dep(dep[b]) for b in range(3)]
+        for b in range(3, 7):
+            round_w1((b - 3) // 2, (b - 3) % 2)
+            if b < 6:
+                sum_picks(b - 3, picks[b - 3])
+            dep.append(dep_window(b))
+            picks.append(pick_dep(dep[b]))
+        sum_picks(3, picks[3])
+        dep.append(dep_window(7))
+        picks.append(pick_dep(dep[7]))
+        den = [den_window(0)]
+        sum_picks(4, picks[4])
+        sum_picks(5, picks[5])
+        den.extend(den_window(t) for t in range(1, 4))
+        turn_back(0)
+        sum_picks(6, picks[6])
+        sum_picks(7, picks[7])
+        turn_back(1)
+        j0 = 0
+        waiting = []
+        for i, width in enumerate(PAIR_CHUNKS):
+            rounded = pick_den(den, j0, width)
+            if i == 0:
+                level_product()
+            for args in waiting:
+                finish(*args)
+            waiting = [(rounded, c0, j0 + c0, j0 + c0 + P == PAIRS) for c0 in range(0, width, P)]
+            j0 = j0 + width
+        for args in waiting:
+            finish(*args)

@@ -20,7 +20,7 @@ ALU = mybir.AluOpType
 P = 128
 BANK = 512
 HALVES = S // BANK
-SPARE_ROW = 112
+SPARE_ROW = 96
 PAIR_CHUNKS = (256, 128, 128)
 
 
@@ -30,8 +30,15 @@ def tile_list_saltpond_transfer_features_kernel(
     nc = tc.nc
     with ExitStack() as ctx:
         keep = ctx.enter_context(tc.tile_pool(name="keep", bufs=1))
-        ring = ctx.enter_context(tc.tile_pool(name="ring", bufs=8))
-        psum = ctx.enter_context(tc.psum_pool(name="psum", bufs=2))
+        ring = ctx.enter_context(tc.tile_pool(name="ring", bufs=16))
+        psum = ctx.enter_context(tc.psum_pool(name="psum", bufs=1))
+
+        used_banks = []
+
+        def next_bank():
+            tag = f"bank{len(used_banks) % 8}"
+            used_banks.append(tag)
+            return psum.tile([P, BANK], F32, name=tag, tag=tag)
 
         def held(shape, dtype, name, tag=None):
             return keep.tile(shape, dtype, name=name, tag=tag or name, align_bytes=64)
@@ -40,61 +47,61 @@ def tile_list_saltpond_transfer_features_kernel(
         pos1_sb = keep.tile([P, PAIRS // 16], U16, name="pos1_sb")
         pos2_sb = keep.tile([P, PAIRS // 16], U16, name="pos2_sb")
         nc.sync.dma_start(offs_sb[:], offs)
-
-        tab_sc = held([P, T], U8, "tab_sc", "early0")
-        nc.sync.dma_start(tab_sc[SPARE_ROW:P, :].bitcast(I32), tab_scales[1].bitcast(I32))
+        tab_sc = held([P, T], U8, "tab_sc")
+        nc.sync.dma_start(tab_sc[SPARE_ROW:P, :].bitcast(I32), tab_scales.rearrange("a q t -> (a q) t").bitcast(I32))
         nc.vector.memset(tab_sc[0:SPARE_ROW, :].bitcast(I32), 0)
-        for q in range(4):
-            nc.scalar.dma_start(tab_sc[32 * q : 32 * q + 4, :].bitcast(I32), tab_scales[0, 4 * q : 4 * q + 4, :].bitcast(I32))
-
-        tab_w = [held([P, T], U16, f"tab_w{a}", f"early{a + 1}") for a in range(2)]
-        nc.sync.dma_start(tab_w[0][:].bitcast(I32), tab_words[0].bitcast(I32))
         nc.sync.dma_start(pos1_sb[:], pos1)
         nc.sync.dma_start(pos2_sb[:], pos2)
-        nc.sync.dma_start(tab_w[1][:].bitcast(I32), tab_words[1].bitcast(I32))
+        tab_w = [held([P, T], U16, f"tab_w{a}", f"chain{a}") for a in range(2)]
+        for a in range(2):
+            nc.sync.dma_start(tab_w[a][:].bitcast(I32), tab_words[a].bitcast(I32))
 
-        w2_c = [held([P, 2, BANK], U32, f"w2_c{g}") for g in range(2)]
         w2_view = w2_words.rearrange("a p c i -> p a (c i)")
-        for g in range(2):
-            nc.sync.dma_start(w2_c[g][:].bitcast(I32), w2_view[:, :, 4 * BANK * g : 4 * BANK * (g + 1)].bitcast(I32))
 
-        def load_scale_planes(planes, scales):
-            nc.gpsimd.memset(planes[:].bitcast(I32), 0)
+        def load_w2(g, tag):
+            codes = held([P, 2, BANK], U32, f"w2_c{g}", tag)
+            nc.sync.dma_start(codes[:].bitcast(I32), w2_view[:, :, 4 * BANK * g : 4 * BANK * (g + 1)].bitcast(I32))
+            return codes
+
+        def load_scale_planes(planes, scales, queue):
             for q in range(4):
-                nc.gpsimd.dma_start(
+                queue.dma_start(
                     planes[32 * q : 32 * q + 4, :, :].bitcast(I32),
                     scales[:, 4 * q : 4 * q + 4, :].rearrange("a r c -> r a c").bitcast(I32),
                 )
 
-        w2_s = held([P, 2, M], U8, "w2_s")
-        load_scale_planes(w2_s, w2_scales)
+        def load_w1(a, tag):
+            raw = held([P, 4, R], F32, f"w1_raw{a}", tag)
+            nc.sync.dma_start(raw[:], w1[512 * a : 512 * (a + 1), :].rearrange("(p j) c -> p j c", j=4))
+            return raw
+
+        w2_c = [load_w2(0, None)]
+        gain_sb = held([P, 4], F32, "gain_sb")
+        nc.sync.dma_start(gain_sb[:], gain.rearrange("(p t) -> p t", t=4))
         ident = held([P, P], F32, "ident")
         make_identity(nc, ident[:])
-        w4_s = held([P, 2, N], U8, "w4_s")
-        load_scale_planes(w4_s, w4_scales)
-        gain_sb = held([P, 4], F32, "gain_sb")
-        nc.gpsimd.dma_start(gain_sb[:], gain.rearrange("(p t) -> p t", t=4))
-        w4_c = held([P, 2, 2 * N], U8, "w4_c")
-        nc.gpsimd.dma_start(w4_c[:].bitcast(I32), w4_words.rearrange("a p c -> p a c").bitcast(I32))
+        w2_s = held([P, 2, M], U8, "w2_s")
+        nc.gpsimd.memset(w2_s[:].bitcast(I32), 0)
+        load_scale_planes(w2_s, w2_scales, nc.gpsimd)
 
         v_s = [held([P, S], U8, f"v_s{a}") for a in range(2)]
-        nc.vector.memset(v_s[1][:].bitcast(I32), 0)
-        nc.vector.tensor_copy(v_s[0][:], tab_sc[:].indirect(offs_sb[:]))
-        for q in range(4):
-            nc.scalar.dma_start(
-                v_s[1][32 * q : 32 * q + 4, :].bitcast(I32),
-                v_s[0][SPARE_ROW + 4 * q : SPARE_ROW + 4 * q + 4, :].bitcast(I32),
-            )
+        for a in range(2):
+            nc.vector.memset(v_s[a][:].bitcast(I32), 0)
+        picked_sc = held([P, S], U8, "picked_sc", "chain2")
+        nc.vector.tensor_copy(picked_sc[:], tab_sc[:].indirect(offs_sb[:]))
+        for a in range(2):
+            for q in range(4):
+                row = SPARE_ROW + 16 * a + 4 * q
+                nc.scalar.dma_start(v_s[a][32 * q : 32 * q + 4, :].bitcast(I32), picked_sc[row : row + 4, :].bitcast(I32))
         v_c = [[held([P, BANK], U16, f"v_c{a}{h}") for h in range(HALVES)] for a in range(2)]
         for a in range(2):
             for h in range(HALVES):
                 nc.vector.tensor_copy(v_c[a][h][:], tab_w[a][:].indirect(offs_sb[:, 32 * h : 32 * (h + 1)]))
 
-        w3_raw = held([P, 4, N], F32, "w3_raw", "early0")
+        w3_raw = held([P, 4, N], F32, "w3_raw", "chain0")
         nc.sync.dma_start(w3_raw[:], w3.rearrange("(p j) n -> p j n", j=4))
-        w1_raw = [held([P, 4, R], F32, f"w1_raw{a}", f"early{a + 1}") for a in range(2)]
-        for a in range(2):
-            nc.sync.dma_start(w1_raw[a][:], w1[512 * a : 512 * (a + 1), :].rearrange("(p j) c -> p j c", j=4))
+        w1_raw = [load_w1(0, "chain2")]
+        w2_c.append(load_w2(1, "chain1"))
 
         w3_b = held([P, 4 * N], BF16, "w3_b")
         w3_c = held([P, N], U32, "w3_c")
@@ -103,6 +110,7 @@ def tile_list_saltpond_transfer_features_kernel(
         for c0, c1 in ((0, 256), (256, N)):
             nc.vector.quantize_mx(w3_c[:, c0:c1].bitcast(E4M3), w3_s[:, c0:c1], w3_b[:, 4 * c0 : 4 * c1])
 
+        w1_raw.append(load_w1(1, "chain0"))
         w1_b = [held([P, 4 * R], BF16, f"w1_b{a}") for a in range(2)]
         w1_c = [held([P, R], U32, f"w1_c{a}") for a in range(2)]
         w1_s = [held([P, R], U8, f"w1_s{a}") for a in range(2)]
@@ -120,7 +128,7 @@ def tile_list_saltpond_transfer_features_kernel(
             window = held([P, S], F32, name)
             for h in range(HALVES):
                 cols = slice(BANK * h, BANK * (h + 1))
-                acc = psum.tile([P, BANK], F32, name="acc", tag="acc", bufs=4)
+                acc = next_bank()
                 for a in range(2):
                     nc.tensor.matmul_mx(
                         acc[:], codes[a].bitcast(E4M3), scales[a], v_c[a][h][:].bitcast(E2M1), v_s[a][:, cols],
@@ -156,7 +164,7 @@ def tile_list_saltpond_transfer_features_kernel(
         both_s = [held([P, PAIRS], U8, f"both_s{g}") for g in range(2)]
 
         def sum_picks(b, picks):
-            bank = psum.tile([P, BANK], F32, name="total", tag="total")
+            bank = next_bank()
             for jb in range(4):
                 cols = slice(P * jb, P * (jb + 1))
                 for i in range(2):
@@ -171,7 +179,7 @@ def tile_list_saltpond_transfer_features_kernel(
             words = both_t[g][:].bitcast(F32)
             dst = both_b[g][:].bitcast(F32)
             for half in range(2):
-                bank = psum.tile([P, BANK], F32, name="back", tag="back")
+                bank = next_bank()
                 for i in range(4):
                     nc.tensor.transpose(bank[:, P * i : P * (i + 1)], words[:, P * (4 * half + i) : P * (4 * half + i + 1)], ident[:])
                 nc.scalar.copy(
@@ -182,9 +190,9 @@ def tile_list_saltpond_transfer_features_kernel(
 
         level = held([P, 3, PAIRS], F32, "level")
 
-        def level_product():
+        def level_product(w4_c, w4_s):
             for nt in range(3):
-                acc = psum.tile([P, BANK], F32, name="acc", tag="acc", bufs=4)
+                acc = next_bank()
                 for g in range(2):
                     nc.tensor.matmul_mx(
                         acc[:], w4_c[:, g, 2 * P * nt : 2 * P * (nt + 1)].bitcast(E2M1), w4_s[:, g, P * nt : P * (nt + 1)],
@@ -195,12 +203,17 @@ def tile_list_saltpond_transfer_features_kernel(
         def pick_den(den, j0, width):
             entries = slice(j0 // 16, (j0 + width) // 16)
             rounded = held([P, 4, width], BF16, f"diff_r{j0}")
-            for t in range(4):
-                taker = ring.tile([P, width], F32, name="taker", tag="taker", bufs=4)
-                diff = ring.tile([P, width], F32, name="diff", tag="diff", bufs=4)
-                nc.vector.tensor_copy(taker[:], den[t][:].indirect(pos2_sb[:, entries]))
-                nc.vector.tensor_tensor(diff[:], den[t][:].indirect(pos1_sb[:, entries]), taker[:], ALU.subtract)
-                nc.scalar.activation(rounded[:, t, :], diff[:], ACT.Copy, scale=gain_sb[:, t : t + 1])
+            takers = []
+            for step in range(5):
+                if step < 4:
+                    taker = ring.tile([P, width], F32, name="taker", tag="taker", bufs=4)
+                    nc.vector.tensor_copy(taker[:], den[step][:].indirect(pos2_sb[:, entries]))
+                    takers.append(taker)
+                if step > 0:
+                    t = step - 1
+                    diff = ring.tile([P, width], F32, name="diff", tag="diff", bufs=4)
+                    nc.vector.tensor_tensor(diff[:], den[t][:].indirect(pos1_sb[:, entries]), takers[t][:], ALU.subtract)
+                    nc.scalar.activation(rounded[:, t, :], diff[:], ACT.Copy, scale=gain_sb[:, t : t + 1])
             return rounded
 
         out_view = out.rearrange("(nt p) j -> p nt j", p=P)
@@ -216,8 +229,7 @@ def tile_list_saltpond_transfer_features_kernel(
             else:
                 nc.scalar.copy(dst, src)
             nc.vector.quantize_mx(codes[:].bitcast(E4M3), scales[:], woven[:])
-            tag = "total" if (j0 // P) % 2 == 0 else "back"
-            drive = psum.tile([P, BANK], F32, name=tag, tag=tag)
+            drive = next_bank()
             for nt in range(3):
                 cols = slice(P * nt, P * (nt + 1))
                 nc.tensor.matmul_mx(
@@ -229,31 +241,33 @@ def tile_list_saltpond_transfer_features_kernel(
             )
             nc.sync.dma_start(out_view[:, :, j0 : j0 + P], result[:])
 
-        dep = [dep_window(0), dep_window(1), dep_window(2)]
-        picks = [pick_dep(dep[b]) for b in range(3)]
-        for b in range(3, 7):
-            round_w1((b - 3) // 2, (b - 3) % 2)
-            if b < 6:
-                sum_picks(b - 3, picks[b - 3])
-            dep.append(dep_window(b))
-            picks.append(pick_dep(dep[b]))
-        sum_picks(3, picks[3])
-        dep.append(dep_window(7))
-        picks.append(pick_dep(dep[7]))
-        den = [den_window(0)]
-        sum_picks(4, picks[4])
-        sum_picks(5, picks[5])
-        den.extend(den_window(t) for t in range(1, 4))
+        picks = []
+        for b in range(8):
+            if b in (4, 6):
+                for half in range(2):
+                    round_w1(b // 2 - 2, half)
+            picks.append(pick_dep(dep_window(b)))
+        w4_c = held([P, 2, 2 * N], U8, "w4_c", "chain2")
+        nc.sync.dma_start(w4_c[:].bitcast(I32), w4_words.rearrange("a p c -> p a c").bitcast(I32))
+        w4_s = held([P, 2, N], U8, "w4_s", "chain0")
+        nc.vector.memset(w4_s[:].bitcast(I32), 0)
+        load_scale_planes(w4_s, w4_scales, nc.sync)
+        den = []
+        for t in range(4):
+            if t % 2 == 0:
+                sum_picks(t, picks[t])
+                sum_picks(t + 1, picks[t + 1])
+            den.append(den_window(t))
         turn_back(0)
-        sum_picks(6, picks[6])
-        sum_picks(7, picks[7])
+        for b in range(4, 8):
+            sum_picks(b, picks[b])
         turn_back(1)
         j0 = 0
         waiting = []
         for i, width in enumerate(PAIR_CHUNKS):
             rounded = pick_den(den, j0, width)
             if i == 0:
-                level_product()
+                level_product(w4_c, w4_s)
             for args in waiting:
                 finish(*args)
             waiting = [(rounded, c0, j0 + c0, j0 + c0 + P == PAIRS) for c0 in range(0, width, P)]

@@ -20,8 +20,7 @@ ALU = mybir.AluOpType
 P = 128
 BANK = 512
 HALVES = S // BANK
-SPARE_ROW = 96
-PAIR_CHUNKS = (256, 128, 128)
+SUM_LAG = 3
 
 
 def tile_list_saltpond_transfer_features_kernel(
@@ -48,8 +47,11 @@ def tile_list_saltpond_transfer_features_kernel(
         pos2_sb = keep.tile([P, PAIRS // 16], U16, name="pos2_sb")
         nc.sync.dma_start(offs_sb[:], offs)
         tab_sc = held([P, T], U8, "tab_sc")
-        nc.sync.dma_start(tab_sc[SPARE_ROW:P, :].bitcast(I32), tab_scales.rearrange("a q t -> (a q) t").bitcast(I32))
-        nc.vector.memset(tab_sc[0:SPARE_ROW, :].bitcast(I32), 0)
+        scale_rows = tab_scales.rearrange("a (h o r) t -> o (a h) r t", h=2, o=2)
+        for o in range(2):
+            nc.sync.dma_start(tab_sc[32 * o + 16 : 32 * o + 32, :].bitcast(I32), scale_rows[o].bitcast(I32))
+        for p0, p1 in ((64, 128), (0, 16), (32, 48)):
+            nc.vector.memset(tab_sc[p0:p1, :].bitcast(I32), 0)
         nc.sync.dma_start(pos1_sb[:], pos1)
         nc.sync.dma_start(pos2_sb[:], pos2)
         tab_w = [held([P, T], U16, f"tab_w{a}", f"chain{a}") for a in range(2)]
@@ -70,14 +72,7 @@ def tile_list_saltpond_transfer_features_kernel(
                     scales[:, 4 * q : 4 * q + 4, :].rearrange("a r c -> r a c").bitcast(I32),
                 )
 
-        def load_w1(a, tag):
-            raw = held([P, 4, R], F32, f"w1_raw{a}", tag)
-            nc.sync.dma_start(raw[:], w1[512 * a : 512 * (a + 1), :].rearrange("(p j) c -> p j c", j=4))
-            return raw
-
-        w2_c = [load_w2(0, None)]
-        gain_sb = held([P, 4], F32, "gain_sb")
-        nc.sync.dma_start(gain_sb[:], gain.rearrange("(p t) -> p t", t=4))
+        w2_c = [load_w2(0, "chain3")]
         ident = held([P, P], F32, "ident")
         make_identity(nc, ident[:])
         w2_s = held([P, 2, M], U8, "w2_s")
@@ -85,44 +80,34 @@ def tile_list_saltpond_transfer_features_kernel(
         load_scale_planes(w2_s, w2_scales, nc.gpsimd)
 
         v_s = [held([P, S], U8, f"v_s{a}") for a in range(2)]
-        for a in range(2):
-            nc.vector.memset(v_s[a][:].bitcast(I32), 0)
         picked_sc = held([P, S], U8, "picked_sc", "chain2")
         nc.vector.tensor_copy(picked_sc[:], tab_sc[:].indirect(offs_sb[:]))
         for a in range(2):
-            for q in range(4):
-                row = SPARE_ROW + 16 * a + 4 * q
-                nc.scalar.dma_start(v_s[a][32 * q : 32 * q + 4, :].bitcast(I32), picked_sc[row : row + 4, :].bitcast(I32))
+            for h in range(2):
+                row = 16 + 8 * a + 4 * h
+                nc.scalar.dma_start(v_s[a][64 * h : 64 * h + 64, :].bitcast(I32), picked_sc[row : row + 64, :].bitcast(I32))
         v_c = [[held([P, BANK], U16, f"v_c{a}{h}") for h in range(HALVES)] for a in range(2)]
         for a in range(2):
             for h in range(HALVES):
                 nc.vector.tensor_copy(v_c[a][h][:], tab_w[a][:].indirect(offs_sb[:, 32 * h : 32 * (h + 1)]))
 
-        w3_raw = held([P, 4, N], F32, "w3_raw", "chain0")
-        nc.sync.dma_start(w3_raw[:], w3.rearrange("(p j) n -> p j n", j=4))
-        w1_raw = [load_w1(0, "chain2")]
+        w1_raw = [held([P, 4 * R], F32, f"w1_raw{a}", f"chain{2 * a}") for a in range(2)]
+        w1_view = w1.rearrange("(a p j) c -> a p (j c)", a=2, j=4)
+        nc.sync.dma_start(w1_raw[0][:], w1_view[0])
         w2_c.append(load_w2(1, "chain1"))
+        nc.sync.dma_start(w1_raw[1][:], w1_view[1])
 
-        w3_b = held([P, 4 * N], BF16, "w3_b")
-        w3_c = held([P, N], U32, "w3_c")
-        w3_s = held([P, N], U8, "w3_s")
-        nc.vector.tensor_copy(w3_b[:].rearrange("p (n j) -> p n j", j=4), w3_raw[:].rearrange("p j n -> p n j"))
-        for c0, c1 in ((0, 256), (256, N)):
-            nc.vector.quantize_mx(w3_c[:, c0:c1].bitcast(E4M3), w3_s[:, c0:c1], w3_b[:, 4 * c0 : 4 * c1])
-
-        w1_raw.append(load_w1(1, "chain0"))
-        w1_b = [held([P, 4 * R], BF16, f"w1_b{a}") for a in range(2)]
+        w1_b = []
         w1_c = [held([P, R], U32, f"w1_c{a}") for a in range(2)]
         w1_s = [held([P, R], U8, f"w1_s{a}") for a in range(2)]
 
-        def round_w1(a, half):
-            rows = slice(64 * half, 64 * (half + 1))
-            nc.scalar.copy(
-                w1_b[a][:].rearrange("p (t m j) -> p m j t", t=4, j=4)[:, rows],
-                w1_raw[a][:].rearrange("p j (m t) -> p m j t", t=4)[:, rows],
-            )
-            if half == 1:
-                nc.vector.quantize_mx(w1_c[a][:].bitcast(E4M3), w1_s[a][:], w1_b[a][:])
+        def round_w1(a):
+            w1_b.append(held([P, 4 * R], BF16, f"w1_b{a}"))
+            src = w1_raw[a][:].rearrange("p (j b t c i) -> p t b c j i", j=4, t=4, c=2, i=4)
+            dst = w1_b[a][:].rearrange("p (t b c i j) -> p t b c j i", t=4, c=2, i=4, j=4)
+            for t in range(4):
+                nc.scalar.copy(dst[:, t], src[:, t])
+            nc.vector.quantize_mx(w1_c[a][:].bitcast(E4M3), w1_s[a][:], w1_b[a][:])
 
         def first_stage(name, codes, scales, func):
             window = held([P, S], F32, name)
@@ -150,18 +135,18 @@ def tile_list_saltpond_transfer_features_kernel(
             cols = slice(P * t, P * (t + 1))
             return first_stage(f"den{t}", [w1_c[a][:, cols] for a in range(2)], [w1_s[a][:, cols] for a in range(2)], ACT.Tanh)
 
-        def pick_dep(window):
+        def pick_dep(b, window):
             picks = []
-            for pos_sb in (pos1_sb, pos2_sb):
-                pick = ring.tile([P, PAIRS], F32, name="pick", tag="pick")
+            for i, pos_sb in enumerate((pos1_sb, pos2_sb)):
+                pick = held([P, PAIRS], F32, f"pick{b}_{i}")
                 nc.vector.tensor_copy(pick[:], window[:].indirect(pos_sb[:]))
                 picks.append(pick)
             return picks
 
         both_t = [held([P, 4 * BANK], BF16, f"both_t{g}") for g in range(2)]
-        both_b = [held([P, 4 * PAIRS], BF16, f"both_b{g}") for g in range(2)]
-        both_c = [held([P, PAIRS], U32, f"both_c{g}") for g in range(2)]
-        both_s = [held([P, PAIRS], U8, f"both_s{g}") for g in range(2)]
+        both_b = held([P, 2 * 4 * PAIRS], BF16, "both_b")
+        both_c = held([P, 2 * PAIRS], U32, "both_c")
+        both_s = held([P, 2 * PAIRS], U8, "both_s")
 
         def sum_picks(b, picks):
             bank = next_bank()
@@ -177,7 +162,7 @@ def tile_list_saltpond_transfer_features_kernel(
 
         def turn_back(g):
             words = both_t[g][:].bitcast(F32)
-            dst = both_b[g][:].bitcast(F32)
+            dst = both_b[:].bitcast(F32)[:, 2 * PAIRS * g : 2 * PAIRS * (g + 1)]
             for half in range(2):
                 bank = next_bank()
                 for i in range(4):
@@ -186,55 +171,52 @@ def tile_list_saltpond_transfer_features_kernel(
                     dst[:, BANK * half : BANK * (half + 1)].rearrange("p (jb j u) -> p jb j u", jb=2, u=2),
                     bank[:].rearrange("p (jb u j) -> p jb j u", jb=2, u=2),
                 )
-            nc.vector.quantize_mx(both_c[g][:].bitcast(E4M3), both_s[g][:], both_b[g][:])
 
         level = held([P, 3, PAIRS], F32, "level")
 
         def level_product(w4_c, w4_s):
+            nc.vector.quantize_mx(both_c[:].bitcast(E4M3), both_s[:], both_b[:])
             for nt in range(3):
                 acc = next_bank()
                 for g in range(2):
+                    cols = slice(PAIRS * g, PAIRS * (g + 1))
                     nc.tensor.matmul_mx(
                         acc[:], w4_c[:, g, 2 * P * nt : 2 * P * (nt + 1)].bitcast(E2M1), w4_s[:, g, P * nt : P * (nt + 1)],
-                        both_c[g][:].bitcast(E4M3), both_s[g][:], start=(g == 0), stop=(g == 1),
+                        both_c[:, cols].bitcast(E4M3), both_s[:, cols], start=(g == 0), stop=(g == 1),
                     )
                 nc.scalar.copy(level[:, nt, :], acc[:])
 
-        def pick_den(den, j0, width):
-            entries = slice(j0 // 16, (j0 + width) // 16)
-            rounded = held([P, 4, width], BF16, f"diff_r{j0}")
-            takers = []
-            for step in range(5):
-                if step < 4:
-                    taker = ring.tile([P, width], F32, name="taker", tag="taker", bufs=4)
-                    nc.vector.tensor_copy(taker[:], den[step][:].indirect(pos2_sb[:, entries]))
-                    takers.append(taker)
-                if step > 0:
-                    t = step - 1
-                    diff = ring.tile([P, width], F32, name="diff", tag="diff", bufs=4)
-                    nc.vector.tensor_tensor(diff[:], den[t][:].indirect(pos1_sb[:, entries]), takers[t][:], ALU.subtract)
-                    nc.scalar.activation(rounded[:, t, :], diff[:], ACT.Copy, scale=gain_sb[:, t : t + 1])
-            return rounded
+        def take(den, j0, width, taker):
+            nc.vector.tensor_copy(taker, den[:].indirect(pos2_sb[:, j0 // 16 : (j0 + width) // 16]))
+
+        def give(den, gain_t, j0, width, taker, rounded):
+            diff = ring.tile([P, width], F32, name="diff", tag="diff")
+            nc.vector.tensor_tensor(diff[:], den[:].indirect(pos1_sb[:, j0 // 16 : (j0 + width) // 16]), taker, ALU.subtract)
+            nc.scalar.activation(rounded, diff[:], ACT.Copy, scale=gain_t[:])
 
         out_view = out.rearrange("(nt p) j -> p nt j", p=P)
 
-        def finish(rounded, c0, j0, last):
+        def quantize_diff(rounded, c0, j0, weave):
             woven = held([P, 4 * P], BF16, f"diff_b{j0}")
             codes = held([P, P], U32, f"diff_c{j0}")
             scales = held([P, P], U8, f"diff_s{j0}")
-            src = rounded[:, :, c0 : c0 + P].rearrange("p t j -> p j t")
-            dst = woven[:].rearrange("p (j t) -> p j t", t=4)
-            if last:
-                nc.vector.tensor_copy(dst, src)
-            else:
-                nc.scalar.copy(dst, src)
+            weave(
+                woven[:].rearrange("p (c i t) -> p c t i", i=4, t=4),
+                rounded[:, :, c0 : c0 + P].rearrange("p t (c i) -> p c t i", i=4),
+            )
             nc.vector.quantize_mx(codes[:].bitcast(E4M3), scales[:], woven[:])
+            return codes, scales
+
+        def drive_product(codes, scales):
             drive = next_bank()
             for nt in range(3):
                 cols = slice(P * nt, P * (nt + 1))
                 nc.tensor.matmul_mx(
                     drive[:, cols], w3_c[:, cols].bitcast(E4M3), w3_s[:, cols], codes[:].bitcast(E4M3), scales[:], start=True, stop=True
                 )
+            return drive
+
+        def finish(drive, j0):
             result = held([P, 3, P], F32, f"result{j0}")
             nc.vector.scalar_tensor_tensor(
                 result[:], level[:, :, j0 : j0 + P], 1.0, drive[:, 0 : 3 * P].rearrange("p (nt j) -> p nt j", nt=3), ALU.add, ALU.mult
@@ -243,34 +225,56 @@ def tile_list_saltpond_transfer_features_kernel(
 
         picks = []
         for b in range(8):
-            if b in (4, 6):
-                for half in range(2):
-                    round_w1(b // 2 - 2, half)
-            picks.append(pick_dep(dep_window(b)))
-        w4_c = held([P, 2, 2 * N], U8, "w4_c", "chain2")
+            if b in (3, 5):
+                round_w1(b // 2 - 1)
+            picks.append(pick_dep(b, dep_window(b)))
+            if b >= SUM_LAG:
+                sum_picks(b - SUM_LAG, picks[b - SUM_LAG])
+        w3_raw = held([P, 4, N], F32, "w3_raw", "chain0")
+        for t in range(4):
+            nc.sync.dma_start(w3_raw[:, t, :], w3.rearrange("(b t i) n -> t b i n", t=4, i=8)[t])
+        w4_c = held([P, 2, 2 * N], U8, "w4_c", "chain3")
         nc.sync.dma_start(w4_c[:].bitcast(I32), w4_words.rearrange("a p c -> p a c").bitcast(I32))
-        w4_s = held([P, 2, N], U8, "w4_s", "chain0")
+        w4_s = held([P, 2, N], U8, "w4_s", "chain1")
         nc.vector.memset(w4_s[:].bitcast(I32), 0)
         load_scale_planes(w4_s, w4_scales, nc.sync)
-        den = []
-        for t in range(4):
-            if t % 2 == 0:
-                sum_picks(t, picks[t])
-                sum_picks(t + 1, picks[t + 1])
-            den.append(den_window(t))
+        gains = [held([P, 1], F32, f"gain{t}", f"dep{4 + t}") for t in range(4)]
+        with nc.allow_non_contiguous_dma(reason="one gain value for each row of a slice"):
+            for t in range(4):
+                nc.sync.dma_start(gains[t][:], gain.rearrange("(b t i o) -> t b i o", t=4, i=8, o=1)[t])
+        w3_b = held([P, 4 * N], BF16, "w3_b")
+        w3_c = held([P, N], U32, "w3_c")
+        w3_s = held([P, N], U8, "w3_s")
+
         turn_back(0)
-        for b in range(4, 8):
-            sum_picks(b, picks[b])
+        den = [den_window(0), den_window(1)]
+        sum_picks(5, picks[5])
+        for t in (2, 3):
+            den.append(den_window(t))
+            sum_picks(4 + t, picks[4 + t])
         turn_back(1)
-        j0 = 0
-        waiting = []
-        for i, width in enumerate(PAIR_CHUNKS):
-            rounded = pick_den(den, j0, width)
-            if i == 0:
-                level_product(w4_c, w4_s)
-            for args in waiting:
-                finish(*args)
-            waiting = [(rounded, c0, j0 + c0, j0 + c0 + P == PAIRS) for c0 in range(0, width, P)]
-            j0 = j0 + width
-        for args in waiting:
-            finish(*args)
+        nc.scalar.copy(w3_b[:].rearrange("p (c i j) -> p c j i", i=4, j=4), w3_raw[:].rearrange("p j (c i) -> p c j i", i=4))
+        for c0, c1 in ((0, 256), (256, N)):
+            nc.vector.quantize_mx(w3_c[:, c0:c1].bitcast(E4M3), w3_s[:, c0:c1], w3_b[:, 4 * c0 : 4 * c1])
+
+        early = held([P, 4, 3 * P], BF16, "early", "both_t1")
+        takers = held([P, 4, 3 * P], F32, "takers")
+        parts = ((0, 2 * P), (2 * P, P))
+        for t in range(4):
+            for j0, width in parts:
+                take(den[t], j0, width, takers[:, t, j0 : j0 + width])
+            for j0, width in parts:
+                give(den[t], gains[t], j0, width, takers[:, t, j0 : j0 + width], early[:, t, j0 : j0 + width])
+        quantized = [quantize_diff(early, P * i, P * i, nc.scalar.copy) for i in range(3)]
+        level_product(w4_c, w4_s)
+        drives = [drive_product(*q) for q in quantized]
+        late = held([P, 4, P], BF16, "late")
+        last_takers = held([P, 4, P], F32, "last_takers", "diff_b0")
+        for step in range(5):
+            if step < 4:
+                take(den[step], 3 * P, P, last_takers[:, step, :])
+            if step > 0:
+                give(den[step - 1], gains[step - 1], 3 * P, P, last_takers[:, step - 1, :], late[:, step - 1, :])
+        for i in range(3):
+            finish(drives[i], P * i)
+        finish(drive_product(*quantize_diff(late, 0, 3 * P, nc.scalar.copy)), 3 * P)

@@ -45,16 +45,17 @@ def tile_list_saltpond_transfer_features_kernel(
         offs_sb = keep.tile([P, S // 16], U16, name="offs_sb")
         pos1_sb = keep.tile([P, PAIRS // 16], U16, name="pos1_sb")
         pos2_sb = keep.tile([P, PAIRS // 16], U16, name="pos2_sb")
-        nc.sync.dma_start(offs_sb[:], offs)
         tab_sc = held([P, T], U8, "tab_sc")
         scale_rows = tab_scales.rearrange("a (h o r) t -> o (a h) r t", h=2, o=2)
         for o in range(2):
             nc.sync.dma_start(tab_sc[32 * o + 16 : 32 * o + 32, :].bitcast(I32), scale_rows[o].bitcast(I32))
+        nc.sync.dma_start(offs_sb[:], offs)
         for p0, p1 in ((64, 128), (0, 16), (32, 48)):
-            nc.vector.memset(tab_sc[p0:p1, :].bitcast(I32), 0)
+            for c0, c1 in ((0, 513), (513, T // 4)):
+                nc.vector.memset(tab_sc[p0:p1, :].bitcast(I32)[:, c0:c1], 0)
         nc.sync.dma_start(pos1_sb[:], pos1)
         nc.sync.dma_start(pos2_sb[:], pos2)
-        tab_w = [held([P, T], U16, f"tab_w{a}", f"chain{a}") for a in range(2)]
+        tab_w = [held([P, T], U16, f"tab_w{a}") for a in range(2)]
         for a in range(2):
             nc.sync.dma_start(tab_w[a][:].bitcast(I32), tab_words[a].bitcast(I32))
 
@@ -72,7 +73,7 @@ def tile_list_saltpond_transfer_features_kernel(
                     scales[:, 4 * q : 4 * q + 4, :].rearrange("a r c -> r a c").bitcast(I32),
                 )
 
-        w2_c = [load_w2(0, "chain3")]
+        w2_c = [load_w2(0, None)]
         ident = held([P, P], F32, "ident")
         make_identity(nc, ident[:])
         w2_s = held([P, 2, M], U8, "w2_s")
@@ -91,11 +92,13 @@ def tile_list_saltpond_transfer_features_kernel(
             for h in range(HALVES):
                 nc.vector.tensor_copy(v_c[a][h][:], tab_w[a][:].indirect(offs_sb[:, 32 * h : 32 * (h + 1)]))
 
-        w1_raw = [held([P, 4 * R], F32, f"w1_raw{a}", f"chain{2 * a}") for a in range(2)]
-        w1_view = w1.rearrange("(a p j) c -> a p (j c)", a=2, j=4)
-        nc.sync.dma_start(w1_raw[0][:], w1_view[0])
-        w2_c.append(load_w2(1, "chain1"))
-        nc.sync.dma_start(w1_raw[1][:], w1_view[1])
+        def load_w1(a, tag):
+            raw = held([P, 4 * R], F32, f"w1_raw{a}", tag)
+            nc.sync.dma_start(raw[:], w1.rearrange("(a p j) c -> a p (j c)", a=2, j=4)[a])
+            return raw
+
+        w1_raw = [load_w1(0, "chain2")]
+        w2_c.append(load_w2(1, "tab_w1"))
 
         w1_b = []
         w1_c = [held([P, R], U32, f"w1_c{a}") for a in range(2)]
@@ -109,17 +112,19 @@ def tile_list_saltpond_transfer_features_kernel(
                 nc.scalar.copy(dst[:, t], src[:, t])
             nc.vector.quantize_mx(w1_c[a][:].bitcast(E4M3), w1_s[a][:], w1_b[a][:])
 
-        def first_stage(name, codes, scales, func):
+        def first_stage(name, codes, scales, func, widths):
             window = held([P, S], F32, name)
-            for h in range(HALVES):
-                cols = slice(BANK * h, BANK * (h + 1))
-                acc = next_bank()
-                for a in range(2):
+            starts = [sum(widths[:i]) for i in range(len(widths))]
+            banks = [next_bank() for width in widths]
+            for a in range(2):
+                for c0, width, bank in zip(starts, widths, banks):
                     nc.tensor.matmul_mx(
-                        acc[:], codes[a].bitcast(E4M3), scales[a], v_c[a][h][:].bitcast(E2M1), v_s[a][:, cols],
+                        bank[:, 0:width], codes[a].bitcast(E4M3), scales[a],
+                        v_c[a][c0 // BANK][:, c0 % BANK : c0 % BANK + width].bitcast(E2M1), v_s[a][:, c0 : c0 + width],
                         start=(a == 0), stop=(a == 1),
                     )
-                nc.scalar.activation(window[:, cols], acc[:], func)
+            for c0, width, bank in zip(starts, widths, banks):
+                nc.scalar.activation(window[:, c0 : c0 + width], bank[:, 0:width], func)
             return window
 
         def dep_window(b):
@@ -129,11 +134,12 @@ def tile_list_saltpond_transfer_features_kernel(
                 [w2_c[g][:, a, c0 : c0 + P] for a in range(2)],
                 [w2_s[:, a, P * b : P * (b + 1)] for a in range(2)],
                 ACT.Relu,
+                (BANK, P, P, P, P) if b == 0 else (BANK, BANK),
             )
 
         def den_window(t):
             cols = slice(P * t, P * (t + 1))
-            return first_stage(f"den{t}", [w1_c[a][:, cols] for a in range(2)], [w1_s[a][:, cols] for a in range(2)], ACT.Tanh)
+            return first_stage(f"den{t}", [w1_c[a][:, cols] for a in range(2)], [w1_s[a][:, cols] for a in range(2)], ACT.Tanh, (BANK, BANK))
 
         def pick_dep(b, window):
             picks = []
@@ -225,17 +231,19 @@ def tile_list_saltpond_transfer_features_kernel(
 
         picks = []
         for b in range(8):
-            if b in (3, 5):
-                round_w1(b // 2 - 1)
+            if b in (4, 5):
+                round_w1(b - 4)
             picks.append(pick_dep(b, dep_window(b)))
             if b >= SUM_LAG:
                 sum_picks(b - SUM_LAG, picks[b - SUM_LAG])
-        w3_raw = held([P, 4, N], F32, "w3_raw", "chain0")
+            if b == 0:
+                w1_raw.append(load_w1(1, "dep0"))
+        w3_raw = held([P, 4, N], F32, "w3_raw", "chain2")
         for t in range(4):
             nc.sync.dma_start(w3_raw[:, t, :], w3.rearrange("(b t i) n -> t b i n", t=4, i=8)[t])
-        w4_c = held([P, 2, 2 * N], U8, "w4_c", "chain3")
+        w4_c = held([P, 2, 2 * N], U8, "w4_c", "pick2_0")
         nc.sync.dma_start(w4_c[:].bitcast(I32), w4_words.rearrange("a p c -> p a c").bitcast(I32))
-        w4_s = held([P, 2, N], U8, "w4_s", "chain1")
+        w4_s = held([P, 2, N], U8, "w4_s", "pick1_0")
         nc.vector.memset(w4_s[:].bitcast(I32), 0)
         load_scale_planes(w4_s, w4_scales, nc.sync)
         gains = [held([P, 1], F32, f"gain{t}", f"dep{4 + t}") for t in range(4)]
@@ -277,4 +285,13 @@ def tile_list_saltpond_transfer_features_kernel(
                 give(den[step - 1], gains[step - 1], 3 * P, P, last_takers[:, step - 1, :], late[:, step - 1, :])
         for i in range(3):
             finish(drives[i], P * i)
-        finish(drive_product(*quantize_diff(late, 0, 3 * P, nc.scalar.copy)), 3 * P)
+        codes, scales = quantize_diff(late, 0, 3 * P, nc.scalar.copy)
+        for nt in range(3):
+            cols = slice(P * nt, P * (nt + 1))
+            drive = next_bank()
+            nc.tensor.matmul_mx(
+                drive[:, 0:P], w3_c[:, cols].bitcast(E4M3), w3_s[:, cols], codes[:].bitcast(E4M3), scales[:], start=True, stop=True
+            )
+            result = held([P, P], F32, f"last{nt}")
+            nc.vector.scalar_tensor_tensor(result[:], level[:, nt, 3 * P : PAIRS], 1.0, drive[:, 0:P], ALU.add, ALU.mult)
+            nc.sync.dma_start(out_view[:, nt, 3 * P : PAIRS], result[:])

from contextlib import ExitStack

import concourse.mybir as mybir
from concourse.masks import make_identity

K, R, M, N, T, S, PAIRS = 1024, 512, 1024, 384, 4096, 1024, 512
FLOPS = 2 * K * (R + M) * S + 2 * (R + M) * N * PAIRS

F32 = mybir.dt.float32
BF16 = mybir.dt.bfloat16
I32 = mybir.dt.int32
U32 = mybir.dt.uint32
U16 = mybir.dt.uint16
U8 = mybir.dt.uint8
E4M3 = mybir.dt.float8_e4m3fn_x4
E2M1 = mybir.dt.float4_e2m1fn_x4
ACT = mybir.ActivationFunctionType
ALU = mybir.AluOpType

P = 128
BANK = 512
HALVES = S // BANK
SUM_LAG = 3


def tile_list_saltpond_transfer_features_kernel(
    tc, tab_words, tab_scales, offs, pos1, pos2, w1, gain, w2_words, w2_scales, w3, w4_words, w4_scales, out
):
    nc = tc.nc
    with ExitStack() as ctx:
        keep = ctx.enter_context(tc.tile_pool(name="keep", bufs=1))
        ring = ctx.enter_context(tc.tile_pool(name="ring", bufs=16))
        psum = ctx.enter_context(tc.psum_pool(name="psum", bufs=1))

        used_banks = []

        def next_bank():
            tag = f"bank{len(used_banks) % 8}"
            used_banks.append(tag)
            return psum.tile([P, BANK], F32, name=tag, tag=tag)

        def held(shape, dtype, name, tag=None):
            return keep.tile(shape, dtype, name=name, tag=tag or name, align_bytes=64)

        offs_sb = keep.tile([P, S // 16], U16, name="offs_sb")
        pos1_sb = keep.tile([P, PAIRS // 16], U16, name="pos1_sb")
        pos2_sb = keep.tile([P, PAIRS // 16], U16, name="pos2_sb")
        tab_sc = held([P, T], U8, "tab_sc")
        scale_rows = tab_scales.rearrange("a (h o r) t -> o (a h) r t", h=2, o=2)
        for o in range(2):
            nc.sync.dma_start(tab_sc[32 * o + 16 : 32 * o + 32, :].bitcast(I32), scale_rows[o].bitcast(I32))
        nc.sync.dma_start(offs_sb[:], offs)
        for p0, p1 in ((64, 128), (0, 16), (32, 48)):
            for c0, c1 in ((0, 513), (513, T // 4)):
                nc.vector.memset(tab_sc[p0:p1, :].bitcast(I32)[:, c0:c1], 0)
        nc.sync.dma_start(pos1_sb[:], pos1)
        nc.sync.dma_start(pos2_sb[:], pos2)
        tab_w = [held([P, T], U16, f"tab_w{a}") for a in range(2)]
        for a in range(2):
            nc.sync.dma_start(tab_w[a][:].bitcast(I32), tab_words[a].bitcast(I32))

        w2_view = w2_words.rearrange("a p c i -> p a (c i)")

        def load_w2(g, tag):
            codes = held([P, 2, BANK], U32, f"w2_c{g}", tag)
            nc.sync.dma_start(codes[:].bitcast(I32), w2_view[:, :, 4 * BANK * g : 4 * BANK * (g + 1)].bitcast(I32))
            return codes

        def load_scale_planes(planes, scales, queue):
            for q in range(4):
                queue.dma_start(
                    planes[32 * q : 32 * q + 4, :, :].bitcast(I32),
                    scales[:, 4 * q : 4 * q + 4, :].rearrange("a r c -> r a c").bitcast(I32),
                )

        w2_c = [load_w2(0, None)]
        ident = held([P, P], F32, "ident")
        make_identity(nc, ident[:])
        w2_s = held([P, 2, M], U8, "w2_s")
        nc.gpsimd.memset(w2_s[:].bitcast(I32), 0)
        load_scale_planes(w2_s, w2_scales, nc.gpsimd)

        v_s = [held([P, S], U8, f"v_s{a}") for a in range(2)]
        picked_sc = held([P, S], U8, "picked_sc", "chain2")
        nc.vector.tensor_copy(picked_sc[:], tab_sc[:].indirect(offs_sb[:]))
        for a in range(2):
            for h in range(2):
                row = 16 + 8 * a + 4 * h
                nc.scalar.dma_start(v_s[a][64 * h : 64 * h + 64, :].bitcast(I32), picked_sc[row : row + 64, :].bitcast(I32))
        v_c = [[held([P, BANK], U16, f"v_c{a}{h}") for h in range(HALVES)] for a in range(2)]
        for a in range(2):
            for h in range(HALVES):
                nc.vector.tensor_copy(v_c[a][h][:], tab_w[a][:].indirect(offs_sb[:, 32 * h : 32 * (h + 1)]))

        def load_w1(a, tag):
            raw = held([P, 4 * R], F32, f"w1_raw{a}", tag)
            nc.sync.dma_start(raw[:], w1.rearrange("(a p j) c -> a p (j c)", a=2, j=4)[a])
            return raw

        w1_raw = [load_w1(0, "chain2")]
        w2_c.append(load_w2(1, "tab_w1"))

        w1_b = []
        w1_c = [held([P, R], U32, f"w1_c{a}") for a in range(2)]
        w1_s = [held([P, R], U8, f"w1_s{a}") for a in range(2)]

        def round_w1(a):
            w1_b.append(held([P, 4 * R], BF16, f"w1_b{a}"))
            src = w1_raw[a][:].rearrange("p (j b t c i) -> p t b c j i", j=4, t=4, c=2, i=4)
            dst = w1_b[a][:].rearrange("p (t b c i j) -> p t b c j i", t=4, c=2, i=4, j=4)
            for t in range(4):
                nc.scalar.copy(dst[:, t], src[:, t])
            nc.vector.quantize_mx(w1_c[a][:].bitcast(E4M3), w1_s[a][:], w1_b[a][:])

        def first_stage(name, codes, scales, func, widths):
            window = held([P, S], F32, name)
            starts = [sum(widths[:i]) for i in range(len(widths))]
            banks = [next_bank() for width in widths]
            for a in range(2):
                for c0, width, bank in zip(starts, widths, banks):
                    nc.tensor.matmul_mx(
                        bank[:, 0:width], codes[a].bitcast(E4M3), scales[a],
                        v_c[a][c0 // BANK][:, c0 % BANK : c0 % BANK + width].bitcast(E2M1), v_s[a][:, c0 : c0 + width],
                        start=(a == 0), stop=(a == 1),
                    )
            for c0, width, bank in zip(starts, widths, banks):
                nc.scalar.activation(window[:, c0 : c0 + width], bank[:, 0:width], func)
            return window

        def dep_window(b):
            g, c0 = b // 4, P * (b % 4)
            return first_stage(
                f"dep{b}",
                [w2_c[g][:, a, c0 : c0 + P] for a in range(2)],
                [w2_s[:, a, P * b : P * (b + 1)] for a in range(2)],
                ACT.Relu,
                (BANK, P, P, P, P) if b == 0 else (BANK, BANK),
            )

        def den_window(t):
            cols = slice(P * t, P * (t + 1))
            return first_stage(f"den{t}", [w1_c[a][:, cols] for a in range(2)], [w1_s[a][:, cols] for a in range(2)], ACT.Tanh, (BANK, BANK))

        def pick_dep(b, window):
            picks = []
            for i, pos_sb in enumerate((pos1_sb, pos2_sb)):
                pick = held([P, PAIRS], F32, f"pick{b}_{i}")
                nc.vector.tensor_copy(pick[:], window[:].indirect(pos_sb[:]))
                picks.append(pick)
            return picks

        both_t = [held([P, 4 * BANK], BF16, f"both_t{g}") for g in range(2)]
        both_b = held([P, 2 * 4 * PAIRS], BF16, "both_b")
        both_c = held([P, 2 * PAIRS], U32, "both_c")
        both_s = held([P, 2 * PAIRS], U8, "both_s")

        def sum_picks(b, picks):
            bank = next_bank()
            for jb in range(4):
                cols = slice(P * jb, P * (jb + 1))
                for i in range(2):
                    nc.tensor.matmul(bank[:, cols], picks[i][:, cols], ident[:], start=(i == 0), stop=(i == 1), is_transpose=True)
            rows = slice(32 * (b % 4), 32 * (b % 4 + 1))
            nc.scalar.copy(
                both_t[b // 4][:].rearrange("p (jb u q e) -> p jb u q e", jb=4, u=2, e=2)[:, :, :, rows, :],
                bank[:].rearrange("p (jb q u e) -> p jb u q e", jb=4, u=2, e=2),
            )

        def turn_back(g):
            words = both_t[g][:].bitcast(F32)
            dst = both_b[:].bitcast(F32)[:, 2 * PAIRS * g : 2 * PAIRS * (g + 1)]
            for half in range(2):
                bank = next_bank()
                for i in range(4):
                    nc.tensor.transpose(bank[:, P * i : P * (i + 1)], words[:, P * (4 * half + i) : P * (4 * half + i + 1)], ident[:])
                nc.scalar.copy(
                    dst[:, BANK * half : BANK * (half + 1)].rearrange("p (jb j u) -> p jb j u", jb=2, u=2),
                    bank[:].rearrange("p (jb u j) -> p jb j u", jb=2, u=2),
                )

        level = held([P, 3, PAIRS], F32, "level")

        def level_product(w4_c, w4_s):
            nc.vector.quantize_mx(both_c[:].bitcast(E4M3), both_s[:], both_b[:])
            for nt in range(3):
                acc = next_bank()
                for g in range(2):
                    cols = slice(PAIRS * g, PAIRS * (g + 1))
                    nc.tensor.matmul_mx(
                        acc[:], w4_c[:, g, 2 * P * nt : 2 * P * (nt + 1)].bitcast(E2M1), w4_s[:, g, P * nt : P * (nt + 1)],
                        both_c[:, cols].bitcast(E4M3), both_s[:, cols], start=(g == 0), stop=(g == 1),
                    )
                nc.scalar.copy(level[:, nt, :], acc[:])

        def take(den, j0, width, taker):
            nc.vector.tensor_copy(taker, den[:].indirect(pos2_sb[:, j0 // 16 : (j0 + width) // 16]))

        def give(den, gain_t, j0, width, taker, rounded):
            diff = ring.tile([P, width], F32, name="diff", tag="diff")
            nc.vector.tensor_tensor(diff[:], den[:].indirect(pos1_sb[:, j0 // 16 : (j0 + width) // 16]), taker, ALU.subtract)
            nc.scalar.activation(rounded, diff[:], ACT.Copy, scale=gain_t[:])

        out_view = out.rearrange("(nt p) j -> p nt j", p=P)

        def quantize_diff(rounded, c0, j0, weave):
            woven = held([P, 4 * P], BF16, f"diff_b{j0}")
            codes = held([P, P], U32, f"diff_c{j0}")
            scales = held([P, P], U8, f"diff_s{j0}")
            weave(
                woven[:].rearrange("p (c i t) -> p c t i", i=4, t=4),
                rounded[:, :, c0 : c0 + P].rearrange("p t (c i) -> p c t i", i=4),
            )
            nc.vector.quantize_mx(codes[:].bitcast(E4M3), scales[:], woven[:])
            return codes, scales

        def drive_product(codes, scales):
            drive = next_bank()
            for nt in range(3):
                cols = slice(P * nt, P * (nt + 1))
                nc.tensor.matmul_mx(
                    drive[:, cols], w3_c[:, cols].bitcast(E4M3), w3_s[:, cols], codes[:].bitcast(E4M3), scales[:], start=True, stop=True
                )
            return drive

        def finish(drive, j0):
            result = held([P, 3, P], F32, f"result{j0}")
            nc.vector.scalar_tensor_tensor(
                result[:], level[:, :, j0 : j0 + P], 1.0, drive[:, 0 : 3 * P].rearrange("p (nt j) -> p nt j", nt=3), ALU.add, ALU.mult
            )
            nc.sync.dma_start(out_view[:, :, j0 : j0 + P], result[:])

        picks = []
        for b in range(8):
            if b in (4, 5):
                round_w1(b - 4)
            picks.append(pick_dep(b, dep_window(b)))
            if b >= SUM_LAG:
                sum_picks(b - SUM_LAG, picks[b - SUM_LAG])
            if b == 0:
                w1_raw.append(load_w1(1, "dep0"))
        w3_raw = held([P, 4, N], F32, "w3_raw", "chain2")
        for t in range(4):
            nc.sync.dma_start(w3_raw[:, t, :], w3.rearrange("(b t i) n -> t b i n", t=4, i=8)[t])
        w4_c = held([P, 2, 2 * N], U8, "w4_c", "pick2_0")
        nc.sync.dma_start(w4_c[:].bitcast(I32), w4_words.rearrange("a p c -> p a c").bitcast(I32))
        w4_s = held([P, 2, N], U8, "w4_s", "pick1_0")
        nc.vector.memset(w4_s[:].bitcast(I32), 0)
        load_scale_planes(w4_s, w4_scales, nc.sync)
        gains = [held([P, 1], F32, f"gain{t}", f"dep{4 + t}") for t in range(4)]
        with nc.allow_non_contiguous_dma(reason="one gain value for each row of a slice"):
            for t in range(4):
                nc.sync.dma_start(gains[t][:], gain.rearrange("(b t i o) -> t b i o", t=4, i=8, o=1)[t])
        w3_b = held([P, 4 * N], BF16, "w3_b")
        w3_c = held([P, N], U32, "w3_c")
        w3_s = held([P, N], U8, "w3_s")

        turn_back(0)
        den = [den_window(0), den_window(1)]
        sum_picks(5, picks[5])
        for t in (2, 3):
            den.append(den_window(t))
            sum_picks(4 + t, picks[4 + t])
        turn_back(1)
        nc.scalar.copy(w3_b[:].rearrange("p (c i j) -> p c j i", i=4, j=4), w3_raw[:].rearrange("p j (c i) -> p c j i", i=4))
        for c0, c1 in ((0, 256), (256, N)):
            nc.vector.quantize_mx(w3_c[:, c0:c1].bitcast(E4M3), w3_s[:, c0:c1], w3_b[:, 4 * c0 : 4 * c1])

        early = held([P, 4, 3 * P], BF16, "early", "both_t1")
        takers = held([P, 4, 3 * P], F32, "takers")
        parts = ((0, 2 * P), (2 * P, P))
        for t in range(4):
            for j0, width in parts:
                take(den[t], j0, width, takers[:, t, j0 : j0 + width])
            for j0, width in parts:
                give(den[t], gains[t], j0, width, takers[:, t, j0 : j0 + width], early[:, t, j0 : j0 + width])
        quantized = [quantize_diff(early, P * i, P * i, nc.scalar.copy) for i in range(3)]
        level_product(w4_c, w4_s)
        drives = [drive_product(*q) for q in quantized]
        late = held([P, 4, P], BF16, "late")
        last_takers = held([P, 4, P], F32, "last_takers", "diff_b0")
        for step in range(5):
            if step < 4:
                take(den[step], 3 * P, P, last_takers[:, step, :])
            if step > 0:
                give(den[step - 1], gains[step - 1], 3 * P, P, last_takers[:, step - 1, :], late[:, step - 1, :])
        for i in range(3):
            finish(drives[i], P * i)
        codes, scales = quantize_diff(late, 0, 3 * P, nc.scalar.copy)
        for nt in range(3):
            cols = slice(P * nt, P * (nt + 1))
            drive = next_bank()
            nc.tensor.matmul_mx(
                drive[:, 0:P], w3_c[:, cols].bitcast(E4M3), w3_s[:, cols], codes[:].bitcast(E4M3), scales[:], start=True, stop=True
            )
            result = held([P, P], F32, f"last{nt}")
            nc.vector.scalar_tensor_tensor(result[:], level[:, nt, 3 * P : PAIRS], 1.0, drive[:, 0:P], ALU.add, ALU.mult)
            nc.sync.dma_start(out_view[:, nt, 3 * P : PAIRS], result[:])
